import numpy as np
import ml_dtypes


def mxq(x, axis, fmt="e4m3"):
    dtype, down = {"e4m3": (ml_dtypes.float8_e4m3fn, 7), "e5m2": (ml_dtypes.float8_e5m2, 14)}[fmt]
    v = np.moveaxis(np.asarray(x, np.float32).astype(ml_dtypes.bfloat16).astype(np.float64), axis, -1)
    blocks = v.reshape(v.shape[:-1] + (-1, 32))
    amax = np.abs(blocks).max(-1, keepdims=True)
    byte = np.maximum(np.where(amax > 0, np.frexp(amax)[1] - 1 + 127, 0) - down, 1)
    scale = np.exp2(byte - 127.0)
    codes = (blocks / scale).astype(np.float32).astype(dtype).astype(np.float64)
    return np.moveaxis((codes * scale).reshape(v.shape), -1, axis)


WIDE = False


def mx_kscale(k, group=512):
    if not WIDE:
        return np.ones(k)
    levels = np.array([18, -18])
    if group != 512:
        return np.exp2(np.random.permutation(np.resize(levels, k // group))).repeat(group)
    if k % 512:
        return np.exp2(np.random.permutation(np.resize(levels, k // 32))).repeat(32)
    a = np.empty((k // 512, 16))
    for p in range(k // 512):
        a[p, :8] = np.random.permutation(np.resize(levels, 8))
        for g in range(8):
            far = levels[np.abs(levels - a[p, g]) >= 10]
            a[p, g + 8] = far[np.random.randint(len(far))]
    return np.exp2(a.ravel()).repeat(32)


def f64(x):
    return np.asarray(x).astype(np.float64)


def bf(x):
    return np.asarray(x, np.float32).astype(ml_dtypes.bfloat16)


def planes(Y):
    r, m = Y.shape
    b = f64(bf(Y)).reshape(r // 32, 32, m)
    amax = np.abs(b).max(1)
    byte = np.clip(np.where(amax > 0, np.frexp(amax)[1] - 1 + 127 - 7, 1), 1, 254)
    codes = (b * np.exp2(127.0 - byte)[:, None, :]).reshape(r, m).astype(np.float32).astype(ml_dtypes.float8_e4m3fn).view(np.uint8)
    words = codes.reshape(r // 512, 128, 4, m).transpose(0, 1, 3, 2)
    return np.ascontiguousarray(words), np.ascontiguousarray(byte.astype(np.uint8).reshape(r // 512, 16, m))


G, D, M, N, K, L = 4, 128, 128, 512, 128, 128


def sgn(shape):
    return np.random.uniform(0.5, 2.0, shape) * np.where(np.random.standard_normal(shape) < 0, -1.0, 1.0)


def setup_inputs():
    n = np.random.standard_normal
    s_d = mx_kscale(D, 0)
    s_m = mx_kscale(M, 0)
    s_k = mx_kscale(K, 0)
    return {
        "h": (n((G, D, N)) * s_d[:, None]).astype(np.float32),
        "w1": (n((G, D, M)) / np.sqrt(D) / s_d[:, None]).astype(np.float32),
        "x1": (n((G, M, N))).astype(np.float32),
        "a1": (sgn((G, M, 1)) * s_m[:, None]).astype(np.float32),
        "w2": (n((G, M, K)) / np.sqrt(M) / s_m[:, None]).astype(np.float32),
        "x2": (n((G, K, N))).astype(np.float32),
        "a2": (sgn((G, K, 1)) * s_k[:, None]).astype(np.float32),
        "w3": (n((G, K, L)) / np.sqrt(K) / s_k[:, None]).astype(np.float32),
        "x3": (n((G, L, N))).astype(np.float32),
    }


def reference(h, w1, x1, a1, w2, x2, a2, w3, x3):
    w1q = mxq(f64(w1), 1, "e4m3")
    hq = mxq(f64(h), 1, "e4m3")
    z1 = w1q.transpose(0, 2, 1) @ hq
    h1 = np.maximum(z1 + f64(x1), 0.0) * f64(a1)
    w2q = mxq(f64(w2), 1, "e4m3")
    h1q = mxq(h1, 1, "e4m3")
    z2 = w2q.transpose(0, 2, 1) @ h1q
    h2 = np.maximum(z2 + f64(x2), 0.0) * f64(a2)
    w3q = mxq(f64(w3), 1, "e4m3")
    h2q = mxq(h2, 1, "e4m3")
    z3 = w3q.transpose(0, 2, 1) @ h2q
    y = np.maximum(z3 + f64(x3), 0.0)
    Y = y.reshape(G * L, N)
    words, scales = planes(Y)
    return Y, words, scales

@@ -1,0 +1,169 @@
+from contextlib import ExitStack
+
+import concourse.mybir as mybir
+
+G, D, N = 4, 128, 512
+FLOPS = 3 * G * 2 * D * D * N
+
+F32 = mybir.dt.float32
+BF16 = mybir.dt.bfloat16
+U32 = mybir.dt.uint32
+I32 = mybir.dt.int32
+U8 = mybir.dt.uint8
+FP8X4 = mybir.dt.float8_e4m3fn_x4
+ALU = mybir.AluOpType
+ACT = mybir.ActivationFunctionType
+
+P = 128
+R = 32
+PACK = 4
+C = 256
+CHUNKS = N // C
+NMM = 128
+
+
+def tile_rows_pl_steps_relu_kernel(tc, h, w1, x1, a1, w2, x2, a2, w3, x3, out_0, out_1, out_2):
+    nc = tc.nc
+
+    with ExitStack() as ctx:
+        sb = ctx.enter_context(tc.tile_pool(name="sb", bufs=1))
+        ps = ctx.enter_context(tc.psum_pool(name="ps", bufs=1))
+
+        def tile(name, shape, dtype):
+            return sb.tile(shape, dtype, name=name, align_bytes=64)
+
+        banks = [[ps.tile([P, 512], F32, name="bank%d_%d" % (c, g)) for g in range(G)] for c in range(CHUNKS)]
+
+        w_raw = [tile("w_raw%d" % s, [P, PACK, D], F32) for s in range(3)]
+        w_bf = [tile("w_bf%d" % s, [P, D, PACK], BF16) for s in range(3)]
+        w_codes = [tile("w_codes%d" % s, [P, D], U32) for s in range(3)]
+        w_scales = [tile("w_scales%d" % s, [P, D], U8) for s in range(3)]
+        a_rows = tile("a_rows", [P, 2, G, R], F32)
+        a_col = tile("a_col", [P, 2, G, R], F32)
+        h_raw = [tile("h_raw%d" % c, [P, PACK, C], F32) for c in range(CHUNKS)]
+        x_sb = [[tile("x%d_%d" % (s, c), [P, G, C], F32) for c in range(CHUNKS)] for s in range(2)]
+        x3_sb = tile("x3_sb", [P, G, N], F32)
+        sums = [[tile("sum%d_%d" % (s, c), [P, G, C], F32) for c in range(CHUNKS)] for s in range(3)]
+        state = [[tile("state%d_%d" % (s, c), [P, G, C], BF16) for c in range(CHUNKS)] for s in range(3)]
+        moved = [[tile("moved%d_%d" % (s, c), [P, PACK, C], BF16) for c in range(CHUNKS)] for s in range(3)]
+        grouped = [[tile("grouped%d_%d" % (s, c), [P, C, PACK], BF16) for c in range(CHUNKS)] for s in range(4)]
+        codes = [[tile("codes%d_%d" % (s, c), [P, C], U32) for c in range(CHUNKS)] for s in range(3)]
+        scales = [[tile("scales%d_%d" % (s, c), [P, C], U8) for c in range(CHUNKS)] for s in range(3)]
+        y_sb = [tile("y%d" % c, [P, G, C], F32) for c in range(CHUNKS)]
+        out_codes = [tile("out_codes%d" % c, [P, C], U32) for c in range(CHUNKS)]
+        out_scales = tile("out_scales", [P, N], U8)
+
+        def cols(c):
+            return slice(c * C, (c + 1) * C)
+
+        def packed_rows(t):
+            return t.rearrange("g (p j) n -> (g p) j n", j=PACK)
+
+        def feature_rows(t):
+            return t.rearrange("g m n -> m g n")
+
+        def interleave(engine, dst, src):
+            out = dst.rearrange("p (c i) j -> p c j i", i=4)
+            in_ = src.rearrange("p j (c i) -> p c j i", i=4)
+            if engine == "vector":
+                nc.vector.tensor_copy(out=out, in_=in_)
+            else:
+                nc.scalar.copy(out=out, in_=in_)
+
+        def quantize(dst_codes, dst_scales, src):
+            nc.vector.quantize_mx(out=dst_codes.bitcast(FP8X4), scales=dst_scales, in_=src.rearrange("p n j -> p (n j)"))
+
+        def products(s, c):
+            for k in range(C // NMM):
+                n_cols = slice(k * NMM, (k + 1) * NMM)
+                for g in range(G):
+                    rows = slice(R * g, R * (g + 1))
+                    nc.tensor.matmul_mx(
+                        out=banks[c][g][:, n_cols],
+                        lhsT=w_codes[s][rows, :].bitcast(FP8X4),
+                        lhsT_scale=w_scales[s][rows, :],
+                        rhs=codes[s][c][rows, n_cols].bitcast(FP8X4),
+                        rhs_scale=scales[s][c][rows, n_cols],
+                        start=True,
+                        stop=True,
+                    )
+
+        def add(s, c, g):
+            x = x3_sb[:, g, cols(c)] if s == 2 else x_sb[s][c][:, g, :]
+            nc.vector.tensor_tensor(out=sums[s][c][:, g, :], in0=banks[c][g][:, 0:C], in1=x, op=ALU.add)
+
+        def rectify(s, c, g):
+            if s == 2:
+                nc.vector.tensor_scalar(out=state[s][c][:, g, :], in0=sums[s][c][:, g, :], scalar1=0.0, scalar2=None, op0=ALU.max)
+            else:
+                nc.vector.tensor_scalar(out=state[s][c][:, g, :], in0=sums[s][c][:, g, :], scalar1=0.0,
+                                        scalar2=a_col[:, s, g, 0:1], op0=ALU.max, op1=ALU.mult)
+            nc.sync.dma_start(out=moved[s][c][R * g:R * (g + 1), :, :], in_=state[s][c][:, g, :])
+
+        def finish(s, c):
+            add(s, c, 0)
+            for g in range(1, G):
+                add(s, c, g)
+                rectify(s, c, g - 1)
+            rectify(s, c, G - 1)
+
+        out_rows = out_0.rearrange("(g l) n -> l g n", g=G)
+        word_rows = out_1[0].rearrange("p n u -> p (n u)").bitcast(I32)
+        scale_rows = out_2[0].bitcast(I32)
+
+        def store_result(c):
+            nc.scalar.activation(out=y_sb[c][:], in_=sums[2][c][:], func=ACT.Relu)
+            nc.scalar.dma_start(out=out_rows[:, :, cols(c)], in_=y_sb[c][:])
+
+        with tc.manual_schedule():
+            nc.gpsimd.memset(a_rows[:], 0.0)
+            for s, a in enumerate((a1, a2)):
+                nc.gpsimd.dma_start(out=a_rows[0:P:R, s, :, :], in_=a.rearrange("g (q i) o -> q g (i o)", i=R))
+            nc.scalar.dma_start(out=w_raw[0][:], in_=packed_rows(w1))
+            nc.scalar.dma_start(out=h_raw[0][:], in_=packed_rows(h)[:, :, cols(0)])
+            nc.scalar.dma_start(out=x_sb[0][0][:], in_=feature_rows(x1)[:, :, cols(0)])
+            nc.scalar.dma_start(out=h_raw[1][:], in_=packed_rows(h)[:, :, cols(1)])
+            nc.scalar.dma_start(out=x_sb[0][1][:], in_=feature_rows(x1)[:, :, cols(1)])
+            nc.scalar.dma_start(out=w_raw[1][:], in_=packed_rows(w2))
+            nc.scalar.dma_start(out=w_raw[2][:], in_=packed_rows(w3))
+            nc.scalar.dma_start(out=x_sb[1][0][:], in_=feature_rows(x2)[:, :, cols(0)])
+
+            nc.vector.transpose(out=a_col[:].rearrange("p s g i -> p (s g i)"), in_=a_rows[:].rearrange("p s g i -> p (s g i)"))
+            interleave("scalar", w_bf[0][:], w_raw[0][:])
+            interleave("vector", grouped[0][0][:], h_raw[0][:])
+            quantize(w_codes[0][:], w_scales[0][:], w_bf[0][:])
+            quantize(codes[0][0][:], scales[0][0][:], grouped[0][0][:])
+            products(0, 0)
+            interleave("scalar", grouped[0][1][:], h_raw[1][:])
+            interleave("scalar", w_bf[1][:], w_raw[1][:])
+            interleave("scalar", w_bf[2][:], w_raw[2][:])
+            finish(0, 0)
+            nc.sync.dma_start(out=x_sb[1][1][:], in_=feature_rows(x2)[:, :, cols(1)])
+            quantize(codes[0][1][:], scales[0][1][:], grouped[0][1][:])
+            products(0, 1)
+            quantize(w_codes[1][:], w_scales[1][:], w_bf[1][:])
+            quantize(w_codes[2][:], w_scales[2][:], w_bf[2][:])
+            finish(0, 1)
+            nc.sync.dma_start(out=x3_sb[:], in_=feature_rows(x3))
+
+            for s in (1, 2):
+                for c in range(CHUNKS):
+                    interleave("scalar", grouped[s][c][:], moved[s - 1][c][:])
+                    if s == 2 and c > 0:
+                        store_result(c - 1)
+                    quantize(codes[s][c][:], scales[s][c][:], grouped[s][c][:])
+                    products(s, c)
+                    finish(s, c)
+            store_result(CHUNKS - 1)
+
+            interleave("vector", grouped[3][0][:], moved[2][0][:])
+            split = 160
+            interleave("scalar", grouped[3][1][:, split:C, :], moved[2][1][:, :, split:C])
+            quantize(out_codes[0][:], out_scales[:, cols(0)], grouped[3][0][:])
+            nc.sync.dma_start(out=word_rows[:, cols(0)], in_=out_codes[0][:].bitcast(I32))
+            interleave("vector", grouped[3][1][:, 0:split, :], moved[2][1][:, :, 0:split])
+            quantize(out_codes[1][:], out_scales[:, cols(1)], grouped[3][1][:])
+            nc.sync.dma_start(out=word_rows[:, cols(1)], in_=out_codes[1][:].bitcast(I32))
+            for q in range(G):
+                queue = nc.sync if q % 2 == 0 else nc.scalar
+                queue.dma_start(out=scale_rows[4 * q:4 * q + 4, :], in_=out_scales[R * q:R * q + 4, :].bitcast(I32))

@@ -41,8 +41,8 @@ def tile_rows_pl_steps_relu_kernel(tc, h, w1, x1, a1, w2, x2, a2, w3, x3, out_0,
         a_rows = tile("a_rows", [P, 2, G, R], F32)
         a_col = tile("a_col", [P, 2, G, R], F32)
         h_raw = [tile("h_raw%d" % c, [P, PACK, C], F32) for c in range(CHUNKS)]
-        x_sb = [[tile("x%d_%d" % (s, c), [P, G, C], F32) for c in range(CHUNKS)] for s in range(2)]
-        x3_sb = tile("x3_sb", [P, G, N], F32)
+        x1_sb = [tile("x1_%d" % c, [P, G, C], F32) for c in range(CHUNKS)]
+        x_sb = [None] + [tile("x%d_sb" % (s + 1), [P, G, N], F32) for s in (1, 2)]
         sums = [[tile("sum%d_%d" % (s, c), [P, G, C], F32) for c in range(CHUNKS)] for s in range(3)]
         state = [[tile("state%d_%d" % (s, c), [P, G, C], BF16) for c in range(CHUNKS)] for s in range(3)]
         moved = [[tile("moved%d_%d" % (s, c), [P, PACK, C], BF16) for c in range(CHUNKS)] for s in range(3)]
@@ -74,10 +74,10 @@ def tile_rows_pl_steps_relu_kernel(tc, h, w1, x1, a1, w2, x2, a2, w3, x3, out_0,
             nc.vector.quantize_mx(out=dst_codes.bitcast(FP8X4), scales=dst_scales, in_=src.rearrange("p n j -> p (n j)"))
 
         def products(s, c):
-            for k in range(C // NMM):
-                n_cols = slice(k * NMM, (k + 1) * NMM)
-                for g in range(G):
-                    rows = slice(R * g, R * (g + 1))
+            for g in range(G):
+                rows = slice(R * g, R * (g + 1))
+                for k in range(C // NMM):
+                    n_cols = slice(k * NMM, (k + 1) * NMM)
                     nc.tensor.matmul_mx(
                         out=banks[c][g][:, n_cols],
                         lhsT=w_codes[s][rows, :].bitcast(FP8X4),
@@ -89,7 +89,7 @@ def tile_rows_pl_steps_relu_kernel(tc, h, w1, x1, a1, w2, x2, a2, w3, x3, out_0,
                     )
 
         def add(s, c, g):
-            x = x3_sb[:, g, cols(c)] if s == 2 else x_sb[s][c][:, g, :]
+            x = x1_sb[c][:, g, :] if s == 0 else x_sb[s][:, g, cols(c)]
             nc.vector.tensor_tensor(out=sums[s][c][:, g, :], in0=banks[c][g][:, 0:C], in1=x, op=ALU.add)
 
         def rectify(s, c, g):
@@ -100,70 +100,83 @@ def tile_rows_pl_steps_relu_kernel(tc, h, w1, x1, a1, w2, x2, a2, w3, x3, out_0,
                                         scalar2=a_col[:, s, g, 0:1], op0=ALU.max, op1=ALU.mult)
             nc.sync.dma_start(out=moved[s][c][R * g:R * (g + 1), :, :], in_=state[s][c][:, g, :])
 
-        def finish(s, c):
+        def finish(s, c, between=None):
             add(s, c, 0)
             for g in range(1, G):
                 add(s, c, g)
+                if g == 9 and between is not None:
+                    between()
                 rectify(s, c, g - 1)
             rectify(s, c, G - 1)
+            if between is not None:
+                between()
+
+        def regroup(s, c, split):
+            src = h_raw[c] if s == 0 else moved[s - 1][c]
+            interleave("scalar", grouped[s][c][:, split:C, :], src[:, :, split:C])
+            if split > 0:
+                interleave("vector", grouped[s][c][:, 0:split, :], src[:, :, 0:split])
+
+        def begin(s, c):
+            regroup(s, c, 128)
+            quantize(codes[s][c][:], scales[s][c][:], grouped[s][c][:])
+            products(s, c)
 
         out_rows = out_0.rearrange("(g l) n -> l g n", g=G)
         word_rows = out_1[0].rearrange("p n u -> p (n u)").bitcast(I32)
         scale_rows = out_2[0].bitcast(I32)
 
         def store_result(c):
-            nc.scalar.activation(out=y_sb[c][:], in_=sums[2][c][:], func=ACT.Relu)
-            nc.scalar.dma_start(out=out_rows[:, :, cols(c)], in_=y_sb[c][:])
+            nc.vector.tensor_scalar(out=y_sb[c][:], in0=sums[2][c][:], scalar1=0.0, scalar2=None, op0=ALU.max)
+            nc.sync.dma_start(out=out_rows[:, :, cols(c)], in_=y_sb[c][:])
+
+        def hand_on(c):
+            quantize(out_codes[c][:], out_scales[:, cols(c)], grouped[3][c][:])
+            nc.scalar.dma_start(out=word_rows[:, cols(c)], in_=out_codes[c][:].bitcast(I32))
 
         with tc.manual_schedule():
             nc.gpsimd.memset(a_rows[:], 0.0)
+            nc.sync.dma_start(out=w_raw[0][:], in_=packed_rows(w1))
+            nc.sync.dma_start(out=h_raw[0][:], in_=packed_rows(h)[:, :, cols(0)])
+            nc.sync.dma_start(out=x1_sb[0][:], in_=feature_rows(x1)[:, :, cols(0)])
             for s, a in enumerate((a1, a2)):
-                nc.gpsimd.dma_start(out=a_rows[0:P:R, s, :, :], in_=a.rearrange("g (q i) o -> q g (i o)", i=R))
-            nc.scalar.dma_start(out=w_raw[0][:], in_=packed_rows(w1))
-            nc.scalar.dma_start(out=h_raw[0][:], in_=packed_rows(h)[:, :, cols(0)])
-            nc.scalar.dma_start(out=x_sb[0][0][:], in_=feature_rows(x1)[:, :, cols(0)])
-            nc.scalar.dma_start(out=h_raw[1][:], in_=packed_rows(h)[:, :, cols(1)])
-            nc.scalar.dma_start(out=x_sb[0][1][:], in_=feature_rows(x1)[:, :, cols(1)])
-            nc.scalar.dma_start(out=w_raw[1][:], in_=packed_rows(w2))
-            nc.scalar.dma_start(out=w_raw[2][:], in_=packed_rows(w3))
-            nc.scalar.dma_start(out=x_sb[1][0][:], in_=feature_rows(x2)[:, :, cols(0)])
+                nc.sync.dma_start(out=a_rows[0:P:R, s, :, :], in_=a.rearrange("g (q i) o -> q g (i o)", i=R))
+            nc.sync.dma_start(out=h_raw[1][:], in_=packed_rows(h)[:, :, cols(1)])
+            nc.sync.dma_start(out=x1_sb[1][:], in_=feature_rows(x1)[:, :, cols(1)])
+            nc.sync.dma_start(out=w_raw[1][:], in_=packed_rows(w2))
 
-            nc.vector.transpose(out=a_col[:].rearrange("p s g i -> p (s g i)"), in_=a_rows[:].rearrange("p s g i -> p (s g i)"))
-            interleave("scalar", w_bf[0][:], w_raw[0][:])
-            interleave("vector", grouped[0][0][:], h_raw[0][:])
+            interleave("vector", w_bf[0][:], w_raw[0][:])
+            regroup(0, 0, 160)
             quantize(w_codes[0][:], w_scales[0][:], w_bf[0][:])
             quantize(codes[0][0][:], scales[0][0][:], grouped[0][0][:])
             products(0, 0)
-            interleave("scalar", grouped[0][1][:], h_raw[1][:])
+            nc.vector.transpose(out=a_col[:].rearrange("p s g i -> p (s g i)"), in_=a_rows[:].rearrange("p s g i -> p (s g i)"))
+            regroup(0, 1, 0)
+            nc.scalar.dma_start(out=x_sb[1][:], in_=feature_rows(x2))
+            nc.scalar.dma_start(out=w_raw[2][:], in_=packed_rows(w3))
             interleave("scalar", w_bf[1][:], w_raw[1][:])
-            interleave("scalar", w_bf[2][:], w_raw[2][:])
             finish(0, 0)
-            nc.sync.dma_start(out=x_sb[1][1][:], in_=feature_rows(x2)[:, :, cols(1)])
             quantize(codes[0][1][:], scales[0][1][:], grouped[0][1][:])
             products(0, 1)
             quantize(w_codes[1][:], w_scales[1][:], w_bf[1][:])
-            quantize(w_codes[2][:], w_scales[2][:], w_bf[2][:])
             finish(0, 1)
-            nc.sync.dma_start(out=x3_sb[:], in_=feature_rows(x3))
-
-            for s in (1, 2):
-                for c in range(CHUNKS):
-                    interleave("scalar", grouped[s][c][:], moved[s - 1][c][:])
-                    if s == 2 and c > 0:
-                        store_result(c - 1)
-                    quantize(codes[s][c][:], scales[s][c][:], grouped[s][c][:])
-                    products(s, c)
-                    finish(s, c)
-            store_result(CHUNKS - 1)
-
-            interleave("vector", grouped[3][0][:], moved[2][0][:])
-            split = 160
-            interleave("scalar", grouped[3][1][:, split:C, :], moved[2][1][:, :, split:C])
-            quantize(out_codes[0][:], out_scales[:, cols(0)], grouped[3][0][:])
-            nc.sync.dma_start(out=word_rows[:, cols(0)], in_=out_codes[0][:].bitcast(I32))
-            interleave("vector", grouped[3][1][:, 0:split, :], moved[2][1][:, :, 0:split])
-            quantize(out_codes[1][:], out_scales[:, cols(1)], grouped[3][1][:])
-            nc.sync.dma_start(out=word_rows[:, cols(1)], in_=out_codes[1][:].bitcast(I32))
+            begin(1, 0)
+            nc.scalar.dma_start(out=x_sb[2][:], in_=feature_rows(x3))
+            interleave("scalar", w_bf[2][:], w_raw[2][:])
+            finish(1, 0)
+            begin(1, 1)
+            quantize(w_codes[2][:], w_scales[2][:], w_bf[2][:])
+            finish(1, 1)
+            begin(2, 0)
+            finish(2, 0)
+            begin(2, 1)
+            store_result(0)
+            regroup(3, 0, 0)
+            finish(2, 1)
+            hand_on(0)
+            store_result(1)
+            regroup(3, 1, 160)
+            hand_on(1)
             for q in range(G):
-                queue = nc.sync if q % 2 == 0 else nc.scalar
+                queue = nc.sync if q < 3 else nc.scalar
                 queue.dma_start(out=scale_rows[4 * q:4 * q + 4, :], in_=out_scales[R * q:R * q + 4, :].bitcast(I32))

@@ -12,14 +12,14 @@ I32 = mybir.dt.int32
 U8 = mybir.dt.uint8
 FP8X4 = mybir.dt.float8_e4m3fn_x4
 ALU = mybir.AluOpType
-ACT = mybir.ActivationFunctionType
 
 P = 128
 R = 32
 PACK = 4
-C = 256
+C = 128
 CHUNKS = N // C
-NMM = 128
+H = 256
+STEPS = 3
 
 
 def tile_rows_pl_steps_relu_kernel(tc, h, w1, x1, a1, w2, x2, a2, w3, x3, out_0, out_1, out_2):
@@ -32,40 +32,48 @@ def tile_rows_pl_steps_relu_kernel(tc, h, w1, x1, a1, w2, x2, a2, w3, x3, out_0,
         def tile(name, shape, dtype):
             return sb.tile(shape, dtype, name=name, align_bytes=64)
 
-        banks = [[ps.tile([P, 512], F32, name="bank%d_%d" % (c, g)) for g in range(G)] for c in range(CHUNKS)]
+        def tiles(name, steps, count, shape, dtype):
+            return [[tile("%s%d_%d" % (name, s, c), shape, dtype) for c in range(count)] for s in range(steps)]
 
-        w_raw = [tile("w_raw%d" % s, [P, PACK, D], F32) for s in range(3)]
-        w_bf = [tile("w_bf%d" % s, [P, D, PACK], BF16) for s in range(3)]
-        w_codes = [tile("w_codes%d" % s, [P, D], U32) for s in range(3)]
-        w_scales = [tile("w_scales%d" % s, [P, D], U8) for s in range(3)]
+        banks = [[ps.tile([P, 512], F32, name="bank%d_%d" % (b, g)) for g in range(G)] for b in range(2)]
+
+        w_raw = [tile("w_raw%d" % s, [P, PACK, D], F32) for s in range(STEPS)]
+        w_bf = [tile("w_bf%d" % s, [P, D, PACK], BF16) for s in range(STEPS)]
+        w_codes = [tile("w_codes%d" % s, [P, D], U32) for s in range(STEPS)]
+        w_scales = [tile("w_scales%d" % s, [P, D], U8) for s in range(STEPS)]
         a_rows = tile("a_rows", [P, 2, G, R], F32)
         a_col = tile("a_col", [P, 2, G, R], F32)
-        h_raw = [tile("h_raw%d" % c, [P, PACK, C], F32) for c in range(CHUNKS)]
-        x1_sb = [tile("x1_%d" % c, [P, G, C], F32) for c in range(CHUNKS)]
-        x_sb = [None] + [tile("x%d_sb" % (s + 1), [P, G, N], F32) for s in (1, 2)]
-        sums = [[tile("sum%d_%d" % (s, c), [P, G, C], F32) for c in range(CHUNKS)] for s in range(3)]
-        state = [[tile("state%d_%d" % (s, c), [P, G, C], BF16) for c in range(CHUNKS)] for s in range(3)]
-        moved = [[tile("moved%d_%d" % (s, c), [P, PACK, C], BF16) for c in range(CHUNKS)] for s in range(3)]
-        grouped = [[tile("grouped%d_%d" % (s, c), [P, C, PACK], BF16) for c in range(CHUNKS)] for s in range(4)]
-        codes = [[tile("codes%d_%d" % (s, c), [P, C], U32) for c in range(CHUNKS)] for s in range(3)]
-        scales = [[tile("scales%d_%d" % (s, c), [P, C], U8) for c in range(CHUNKS)] for s in range(3)]
-        y_sb = [tile("y%d" % c, [P, G, C], F32) for c in range(CHUNKS)]
-        out_codes = [tile("out_codes%d" % c, [P, C], U32) for c in range(CHUNKS)]
+        h_raw = [tile("h_raw%d" % i, [P, PACK, H], F32) for i in range(2)]
+        x_sb = tiles("x", STEPS, 2, [P, G, H], F32)
+        sums = tiles("sum", STEPS, 2, [P, G, H], F32)
+        state = tiles("state", STEPS, CHUNKS, [P, G, C], BF16)
+        moved = tiles("moved", STEPS, CHUNKS, [P, PACK, C], BF16)
+        grouped = tiles("grouped", STEPS + 1, CHUNKS, [P, C, PACK], BF16)
+        codes = tiles("codes", STEPS, CHUNKS, [P, C], U32)
+        scales = tiles("scales", STEPS, CHUNKS, [P, C], U8)
+        y_sb = [tile("y%d" % i, [P, G, H], F32) for i in range(2)]
+        out_codes = [tile("out_codes%d" % i, [P, H], U32) for i in range(2)]
         out_scales = tile("out_scales", [P, N], U8)
 
-        def cols(c):
-            return slice(c * C, (c + 1) * C)
+        def half(i):
+            return slice(i * H, (i + 1) * H)
+
+        def within(c):
+            return slice((c % 2) * C, (c % 2 + 1) * C)
 
         def packed_rows(t):
             return t.rearrange("g (p j) n -> (g p) j n", j=PACK)
 
-        def feature_rows(t):
-            return t.rearrange("g m n -> m g n")
+        def load_x(s, i):
+            nc.scalar.dma_start(out=x_sb[s][i][:], in_=(x1, x2, x3)[s].rearrange("g m n -> m g n")[:, :, half(i)])
 
-        def interleave(engine, dst, src):
+        def load_w(s):
+            nc.scalar.dma_start(out=w_raw[s][:], in_=packed_rows((w1, w2, w3)[s]))
+
+        def interleave(on_vector, dst, src):
             out = dst.rearrange("p (c i) j -> p c j i", i=4)
             in_ = src.rearrange("p j (c i) -> p c j i", i=4)
-            if engine == "vector":
+            if on_vector:
                 nc.vector.tensor_copy(out=out, in_=in_)
             else:
                 nc.scalar.copy(out=out, in_=in_)
@@ -73,110 +81,114 @@ def tile_rows_pl_steps_relu_kernel(tc, h, w1, x1, a1, w2, x2, a2, w3, x3, out_0,
         def quantize(dst_codes, dst_scales, src):
             nc.vector.quantize_mx(out=dst_codes.bitcast(FP8X4), scales=dst_scales, in_=src.rearrange("p n j -> p (n j)"))
 
-        def products(s, c):
-            for g in range(G):
-                rows = slice(R * g, R * (g + 1))
-                for k in range(C // NMM):
-                    n_cols = slice(k * NMM, (k + 1) * NMM)
-                    nc.tensor.matmul_mx(
-                        out=banks[c][g][:, n_cols],
-                        lhsT=w_codes[s][rows, :].bitcast(FP8X4),
-                        lhsT_scale=w_scales[s][rows, :],
-                        rhs=codes[s][c][rows, n_cols].bitcast(FP8X4),
-                        rhs_scale=scales[s][c][rows, n_cols],
-                        start=True,
-                        stop=True,
-                    )
-
-        def add(s, c, g):
-            x = x1_sb[c][:, g, :] if s == 0 else x_sb[s][:, g, cols(c)]
-            nc.vector.tensor_tensor(out=sums[s][c][:, g, :], in0=banks[c][g][:, 0:C], in1=x, op=ALU.add)
-
-        def rectify(s, c, g):
-            if s == 2:
-                nc.vector.tensor_scalar(out=state[s][c][:, g, :], in0=sums[s][c][:, g, :], scalar1=0.0, scalar2=None, op0=ALU.max)
-            else:
-                nc.vector.tensor_scalar(out=state[s][c][:, g, :], in0=sums[s][c][:, g, :], scalar1=0.0,
-                                        scalar2=a_col[:, s, g, 0:1], op0=ALU.max, op1=ALU.mult)
-            nc.sync.dma_start(out=moved[s][c][R * g:R * (g + 1), :, :], in_=state[s][c][:, g, :])
-
-        def finish(s, c, between=None):
-            add(s, c, 0)
-            for g in range(1, G):
-                add(s, c, g)
-                if g == 9 and between is not None:
-                    between()
-                rectify(s, c, g - 1)
-            rectify(s, c, G - 1)
-            if between is not None:
-                between()
-
-        def regroup(s, c, split):
-            src = h_raw[c] if s == 0 else moved[s - 1][c]
-            interleave("scalar", grouped[s][c][:, split:C, :], src[:, :, split:C])
-            if split > 0:
-                interleave("vector", grouped[s][c][:, 0:split, :], src[:, :, 0:split])
-
-        def begin(s, c):
-            regroup(s, c, 128)
-            quantize(codes[s][c][:], scales[s][c][:], grouped[s][c][:])
-            products(s, c)
-
         out_rows = out_0.rearrange("(g l) n -> l g n", g=G)
         word_rows = out_1[0].rearrange("p n u -> p (n u)").bitcast(I32)
         scale_rows = out_2[0].bitcast(I32)
 
-        def store_result(c):
-            nc.vector.tensor_scalar(out=y_sb[c][:], in0=sums[2][c][:], scalar1=0.0, scalar2=None, op0=ALU.max)
-            nc.sync.dma_start(out=out_rows[:, :, cols(c)], in_=y_sb[c][:])
+        def regroup(u, on_vector=False):
+            s, c = divmod(u, CHUNKS)
+            src = h_raw[c // 2][:, :, within(c)] if s == 0 else moved[s - 1][c][:]
+            interleave(on_vector, grouped[s][c][:], src)
 
-        def hand_on(c):
-            quantize(out_codes[c][:], out_scales[:, cols(c)], grouped[3][c][:])
-            nc.scalar.dma_start(out=word_rows[:, cols(c)], in_=out_codes[c][:].bitcast(I32))
+        def begin(u):
+            s, c = divmod(u, CHUNKS)
+            if s == STEPS:
+                quantize(out_codes[c // 2][:, within(c)], out_scales[:, c * C:(c + 1) * C], grouped[s][c][:])
+                if c % 2 == 1:
+                    nc.scalar.dma_start(out=word_rows[:, half(c // 2)], in_=out_codes[c // 2][:].bitcast(I32))
+                return
+            quantize(codes[s][c][:], scales[s][c][:], grouped[s][c][:])
+            for g in range(G):
+                rows = slice(R * g, R * (g + 1))
+                nc.tensor.matmul_mx(
+                    out=banks[c % 2][g][:, 0:C],
+                    lhsT=w_codes[s][rows, :].bitcast(FP8X4),
+                    lhsT_scale=w_scales[s][rows, :],
+                    rhs=codes[s][c][rows, :].bitcast(FP8X4),
+                    rhs_scale=scales[s][c][rows, :],
+                    start=True,
+                    stop=True,
+                )
+
+        def add(s, c, g):
+            nc.vector.tensor_tensor(out=sums[s][c // 2][:, g, within(c)], in0=banks[c % 2][g][:, 0:C],
+                                    in1=x_sb[s][c // 2][:, g, within(c)], op=ALU.add)
+
+        def rectify(s, c, g):
+            if s < STEPS - 1:
+                heads = [g]
+                nc.vector.tensor_scalar(out=state[s][c][:, g, :], in0=sums[s][c // 2][:, g, within(c)], scalar1=0.0,
+                                        scalar2=a_col[:, s, g, 0:1], op0=ALU.max, op1=ALU.mult)
+            elif g % 2 == 1:
+                heads = [g - 1, g]
+                nc.vector.tensor_scalar(out=state[s][c][:, g - 1:g + 1, :], in0=sums[s][c // 2][:, g - 1:g + 1, within(c)],
+                                        scalar1=0.0, scalar2=None, op0=ALU.max)
+            else:
+                heads = []
+            for k in heads:
+                nc.sync.dma_start(out=moved[s][c][R * k:R * (k + 1), :, :], in_=state[s][c][:, k, :])
+
+        def finish(u):
+            s, c = divmod(u, CHUNKS)
+            add(s, c, 0)
+            for g in range(1, G):
+                add(s, c, g)
+                if g == 1:
+                    begin(u + 1)
+                rectify(s, c, g - 1)
+            rectify(s, c, G - 1)
+
+        def store_result(i):
+            nc.vector.tensor_scalar(out=y_sb[i][:], in0=sums[STEPS - 1][i][:], scalar1=0.0, scalar2=None, op0=ALU.max)
+            nc.sync.dma_start(out=out_rows[:, :, half(i)], in_=y_sb[i][:])
+
+        def prepare_w(s):
+            interleave(False, w_bf[s][:], w_raw[s][:])
+
+        def quantize_w(s):
+            quantize(w_codes[s][:], w_scales[s][:], w_bf[s][:])
 
         with tc.manual_schedule():
             nc.gpsimd.memset(a_rows[:], 0.0)
-            nc.sync.dma_start(out=w_raw[0][:], in_=packed_rows(w1))
-            nc.sync.dma_start(out=h_raw[0][:], in_=packed_rows(h)[:, :, cols(0)])
-            nc.sync.dma_start(out=x1_sb[0][:], in_=feature_rows(x1)[:, :, cols(0)])
+            load_w(0)
+            nc.scalar.dma_start(out=h_raw[0][:], in_=packed_rows(h)[:, :, half(0)])
+            load_x(0, 0)
             for s, a in enumerate((a1, a2)):
-                nc.sync.dma_start(out=a_rows[0:P:R, s, :, :], in_=a.rearrange("g (q i) o -> q g (i o)", i=R))
-            nc.sync.dma_start(out=h_raw[1][:], in_=packed_rows(h)[:, :, cols(1)])
-            nc.sync.dma_start(out=x1_sb[1][:], in_=feature_rows(x1)[:, :, cols(1)])
-            nc.sync.dma_start(out=w_raw[1][:], in_=packed_rows(w2))
+                nc.scalar.dma_start(out=a_rows[0:P:R, s, :, :], in_=a.rearrange("g (q i) o -> q g (i o)", i=R))
+            nc.scalar.dma_start(out=h_raw[1][:], in_=packed_rows(h)[:, :, half(1)])
+            load_x(0, 1)
+            load_w(1)
 
-            interleave("vector", w_bf[0][:], w_raw[0][:])
-            regroup(0, 0, 160)
-            quantize(w_codes[0][:], w_scales[0][:], w_bf[0][:])
-            quantize(codes[0][0][:], scales[0][0][:], grouped[0][0][:])
-            products(0, 0)
+            interleave(True, w_bf[0][:], w_raw[0][:])
+            regroup(0, True)
+            quantize_w(0)
+            regroup(1)
+            begin(0)
             nc.vector.transpose(out=a_col[:].rearrange("p s g i -> p (s g i)"), in_=a_rows[:].rearrange("p s g i -> p (s g i)"))
-            regroup(0, 1, 0)
-            nc.scalar.dma_start(out=x_sb[1][:], in_=feature_rows(x2))
-            nc.scalar.dma_start(out=w_raw[2][:], in_=packed_rows(w3))
-            interleave("scalar", w_bf[1][:], w_raw[1][:])
-            finish(0, 0)
-            quantize(codes[0][1][:], scales[0][1][:], grouped[0][1][:])
-            products(0, 1)
-            quantize(w_codes[1][:], w_scales[1][:], w_bf[1][:])
-            finish(0, 1)
-            begin(1, 0)
-            nc.scalar.dma_start(out=x_sb[2][:], in_=feature_rows(x3))
-            interleave("scalar", w_bf[2][:], w_raw[2][:])
-            finish(1, 0)
-            begin(1, 1)
-            quantize(w_codes[2][:], w_scales[2][:], w_bf[2][:])
-            finish(1, 1)
-            begin(2, 0)
-            finish(2, 0)
-            begin(2, 1)
-            store_result(0)
-            regroup(3, 0, 0)
-            finish(2, 1)
-            hand_on(0)
+            late = {1: lambda: load_x(1, 0), 2: lambda: load_w(2), 3: lambda: load_x(1, 1),
+                    5: lambda: load_x(2, 0), 7: lambda: load_x(2, 1)}
+            last = (STEPS + 1) * CHUNKS - 1
+            for u in range(STEPS * CHUNKS):
+                regroup(u + 2)
+                if u == 1:
+                    prepare_w(1)
+                if u == 5:
+                    prepare_w(2)
+                finish(u)
+                if u in late:
+                    late[u]()
+                if u == 2:
+                    quantize_w(1)
+                if u == 6:
+                    quantize_w(2)
+                if u == 9:
+                    store_result(0)
+            begin(last - 2)
             store_result(1)
-            regroup(3, 1, 160)
-            hand_on(1)
+            regroup(last - 1)
+            begin(last - 1)
+            regroup(last, True)
+            begin(last)
             for q in range(G):
                 queue = nc.sync if q < 3 else nc.scalar
                 queue.dma_start(out=scale_rows[4 * q:4 * q + 4, :], in_=out_scales[R * q:R * q + 4, :].bitcast(I32))

@@ -18,8 +18,9 @@ R = 32
 PACK = 4
 C = 128
 CHUNKS = N // C
-H = 256
+H = 2 * C
 STEPS = 3
+BANK = 512
 
 
 def tile_rows_pl_steps_relu_kernel(tc, h, w1, x1, a1, w2, x2, a2, w3, x3, out_0, out_1, out_2):
@@ -35,7 +36,7 @@ def tile_rows_pl_steps_relu_kernel(tc, h, w1, x1, a1, w2, x2, a2, w3, x3, out_0,
         def tiles(name, steps, count, shape, dtype):
             return [[tile("%s%d_%d" % (name, s, c), shape, dtype) for c in range(count)] for s in range(steps)]
 
-        banks = [[ps.tile([P, 512], F32, name="bank%d_%d" % (b, g)) for g in range(G)] for b in range(2)]
+        banks = [[ps.tile([P, BANK], F32, name="bank%d_%d" % (b, g)) for g in range(G)] for b in range(2)]
 
         w_raw = [tile("w_raw%d" % s, [P, PACK, D], F32) for s in range(STEPS)]
         w_bf = [tile("w_bf%d" % s, [P, D, PACK], BF16) for s in range(STEPS)]
@@ -71,8 +72,8 @@ def tile_rows_pl_steps_relu_kernel(tc, h, w1, x1, a1, w2, x2, a2, w3, x3, out_0,
             nc.scalar.dma_start(out=w_raw[s][:], in_=packed_rows((w1, w2, w3)[s]))
 
         def interleave(on_vector, dst, src):
-            out = dst.rearrange("p (c i) j -> p c j i", i=4)
-            in_ = src.rearrange("p j (c i) -> p c j i", i=4)
+            out = dst.rearrange("p (b i) j -> p b j i", i=4)
+            in_ = src.rearrange("p j (b i) -> p b j i", i=4)
             if on_vector:
                 nc.vector.tensor_copy(out=out, in_=in_)
             else:
@@ -114,42 +115,34 @@ def tile_rows_pl_steps_relu_kernel(tc, h, w1, x1, a1, w2, x2, a2, w3, x3, out_0,
             nc.vector.tensor_tensor(out=sums[s][c // 2][:, g, within(c)], in0=banks[c % 2][g][:, 0:C],
                                     in1=x_sb[s][c // 2][:, g, within(c)], op=ALU.add)
 
-        def rectify(s, c, g):
-            if s < STEPS - 1:
-                heads = [g]
-                nc.vector.tensor_scalar(out=state[s][c][:, g, :], in0=sums[s][c // 2][:, g, within(c)], scalar1=0.0,
-                                        scalar2=a_col[:, s, g, 0:1], op0=ALU.max, op1=ALU.mult)
-            elif g % 2 == 1:
-                heads = [g - 1, g]
-                nc.vector.tensor_scalar(out=state[s][c][:, g - 1:g + 1, :], in0=sums[s][c // 2][:, g - 1:g + 1, within(c)],
-                                        scalar1=0.0, scalar2=None, op0=ALU.max)
-            else:
-                heads = []
-            for k in heads:
-                nc.sync.dma_start(out=moved[s][c][R * k:R * (k + 1), :, :], in_=state[s][c][:, k, :])
+        def move(s, c, g):
+            nc.sync.dma_start(out=moved[s][c][R * g:R * (g + 1), :, :], in_=state[s][c][:, g, :])
 
         def finish(u):
             s, c = divmod(u, CHUNKS)
-            add(s, c, 0)
-            for g in range(1, G):
+            for g in range(G - 1):
                 add(s, c, g)
-                if g == 1:
-                    begin(u + 1)
-                rectify(s, c, g - 1)
-            rectify(s, c, G - 1)
+            begin(u + 1)
+            add(s, c, G - 1)
+            if s < STEPS - 1:
+                for g in range(G):
+                    nc.vector.tensor_scalar(out=state[s][c][:, g, :], in0=sums[s][c // 2][:, g, within(c)], scalar1=0.0,
+                                            scalar2=a_col[:, s, g, 0:1], op0=ALU.max, op1=ALU.mult)
+                    move(s, c, g)
+            else:
+                for g in range(0, G, 2):
+                    nc.vector.tensor_scalar(out=state[s][c][:, g:g + 2, :], in0=sums[s][c // 2][:, g:g + 2, within(c)],
+                                            scalar1=0.0, scalar2=None, op0=ALU.max)
+                    move(s, c, g)
+                    move(s, c, g + 1)
 
         def store_result(i):
             nc.vector.tensor_scalar(out=y_sb[i][:], in0=sums[STEPS - 1][i][:], scalar1=0.0, scalar2=None, op0=ALU.max)
             nc.sync.dma_start(out=out_rows[:, :, half(i)], in_=y_sb[i][:])
 
-        def prepare_w(s):
-            interleave(False, w_bf[s][:], w_raw[s][:])
-
-        def quantize_w(s):
-            quantize(w_codes[s][:], w_scales[s][:], w_bf[s][:])
-
         with tc.manual_schedule():
-            nc.gpsimd.memset(a_rows[:], 0.0)
+            nc.vector.memset(a_rows[:], 0.0)
+
             load_w(0)
             nc.scalar.dma_start(out=h_raw[0][:], in_=packed_rows(h)[:, :, half(0)])
             load_x(0, 0)
@@ -161,34 +154,34 @@ def tile_rows_pl_steps_relu_kernel(tc, h, w1, x1, a1, w2, x2, a2, w3, x3, out_0,
 
             interleave(True, w_bf[0][:], w_raw[0][:])
             regroup(0, True)
-            quantize_w(0)
+            quantize(w_codes[0][:], w_scales[0][:], w_bf[0][:])
             regroup(1)
             begin(0)
             nc.vector.transpose(out=a_col[:].rearrange("p s g i -> p (s g i)"), in_=a_rows[:].rearrange("p s g i -> p (s g i)"))
-            late = {1: lambda: load_x(1, 0), 2: lambda: load_w(2), 3: lambda: load_x(1, 1),
-                    5: lambda: load_x(2, 0), 7: lambda: load_x(2, 1)}
-            last = (STEPS + 1) * CHUNKS - 1
+
+            preloads = {0: lambda: load_x(1, 0), 1: lambda: load_w(2), 2: lambda: load_x(1, 1),
+                        3: lambda: load_x(2, 0), 5: lambda: load_x(2, 1)}
+
             for u in range(STEPS * CHUNKS):
+                s, c = divmod(u, CHUNKS)
                 regroup(u + 2)
-                if u == 1:
-                    prepare_w(1)
-                if u == 5:
-                    prepare_w(2)
+                if s < STEPS - 1 and c == 1:
+                    interleave(False, w_bf[s + 1][:], w_raw[s + 1][:])
                 finish(u)
-                if u in late:
-                    late[u]()
-                if u == 2:
-                    quantize_w(1)
-                if u == 6:
-                    quantize_w(2)
-                if u == 9:
-                    store_result(0)
+                if u in preloads:
+                    preloads[u]()
+                if s < STEPS - 1 and c == 2:
+                    quantize(w_codes[s + 1][:], w_scales[s + 1][:], w_bf[s + 1][:])
+
+            last = (STEPS + 1) * CHUNKS - 1
             begin(last - 2)
-            store_result(1)
+            store_result(0)
             regroup(last - 1)
             begin(last - 1)
+            store_result(1)
             regroup(last, True)
             begin(last)
-            for q in range(G):
-                queue = nc.sync if q < 3 else nc.scalar
-                queue.dma_start(out=scale_rows[4 * q:4 * q + 4, :], in_=out_scales[R * q:R * q + 4, :].bitcast(I32))
+
+            for g in range(G):
+                queue = nc.sync if g < G - 1 else nc.scalar
+                queue.dma_start(out=scale_rows[PACK * g:PACK * (g + 1), :], in_=out_scales[R * g:R * g + PACK, :].bitcast(I32))

from contextlib import ExitStack

import concourse.mybir as mybir

G, D, N = 4, 128, 512
FLOPS = 3 * G * 2 * D * D * N

F32 = mybir.dt.float32
BF16 = mybir.dt.bfloat16
U32 = mybir.dt.uint32
I32 = mybir.dt.int32
U8 = mybir.dt.uint8
FP8X4 = mybir.dt.float8_e4m3fn_x4
ALU = mybir.AluOpType

P = 128
R = 32
PACK = 4
C = 128
CHUNKS = N // C
H = 2 * C
STEPS = 3
BANK = 512


def tile_rows_pl_steps_relu_kernel(tc, h, w1, x1, a1, w2, x2, a2, w3, x3, out_0, out_1, out_2):
    nc = tc.nc

    with ExitStack() as ctx:
        sb = ctx.enter_context(tc.tile_pool(name="sb", bufs=1))
        ps = ctx.enter_context(tc.psum_pool(name="ps", bufs=1))

        def tile(name, shape, dtype):
            return sb.tile(shape, dtype, name=name, align_bytes=64)

        def tiles(name, steps, count, shape, dtype):
            return [[tile("%s%d_%d" % (name, s, c), shape, dtype) for c in range(count)] for s in range(steps)]

        banks = [[ps.tile([P, BANK], F32, name="bank%d_%d" % (b, g)) for g in range(G)] for b in range(2)]

        w_raw = [tile("w_raw%d" % s, [P, PACK, D], F32) for s in range(STEPS)]
        w_bf = [tile("w_bf%d" % s, [P, D, PACK], BF16) for s in range(STEPS)]
        w_codes = [tile("w_codes%d" % s, [P, D], U32) for s in range(STEPS)]
        w_scales = [tile("w_scales%d" % s, [P, D], U8) for s in range(STEPS)]
        a_rows = tile("a_rows", [P, 2, G, R], F32)
        a_col = tile("a_col", [P, 2, G, R], F32)
        h_raw = [tile("h_raw%d" % i, [P, PACK, H], F32) for i in range(2)]
        x_sb = tiles("x", STEPS, 2, [P, G, H], F32)
        sums = tiles("sum", STEPS, 2, [P, G, H], F32)
        state = tiles("state", STEPS, CHUNKS, [P, G, C], BF16)
        moved = tiles("moved", STEPS, CHUNKS, [P, PACK, C], BF16)
        grouped = tiles("grouped", STEPS + 1, CHUNKS, [P, C, PACK], BF16)
        codes = tiles("codes", STEPS, CHUNKS, [P, C], U32)
        scales = tiles("scales", STEPS, CHUNKS, [P, C], U8)
        y_sb = [tile("y%d" % i, [P, G, H], F32) for i in range(2)]
        out_codes = [tile("out_codes%d" % i, [P, H], U32) for i in range(2)]
        out_scales = tile("out_scales", [P, N], U8)

        def half(i):
            return slice(i * H, (i + 1) * H)

        def within(c):
            return slice((c % 2) * C, (c % 2 + 1) * C)

        def packed_rows(t):
            return t.rearrange("g (p j) n -> (g p) j n", j=PACK)

        def load_x(s, i):
            nc.scalar.dma_start(out=x_sb[s][i][:], in_=(x1, x2, x3)[s].rearrange("g m n -> m g n")[:, :, half(i)])

        def load_w(s):
            nc.scalar.dma_start(out=w_raw[s][:], in_=packed_rows((w1, w2, w3)[s]))

        def interleave(on_vector, dst, src):
            out = dst.rearrange("p (b i) j -> p b j i", i=4)
            in_ = src.rearrange("p j (b i) -> p b j i", i=4)
            if on_vector:
                nc.vector.tensor_copy(out=out, in_=in_)
            else:
                nc.scalar.copy(out=out, in_=in_)

        def quantize(dst_codes, dst_scales, src):
            nc.vector.quantize_mx(out=dst_codes.bitcast(FP8X4), scales=dst_scales, in_=src.rearrange("p n j -> p (n j)"))

        out_rows = out_0.rearrange("(g l) n -> l g n", g=G)
        word_rows = out_1[0].rearrange("p n u -> p (n u)").bitcast(I32)
        scale_rows = out_2[0].bitcast(I32)

        def regroup(u, on_vector=False):
            s, c = divmod(u, CHUNKS)
            src = h_raw[c // 2][:, :, within(c)] if s == 0 else moved[s - 1][c][:]
            interleave(on_vector, grouped[s][c][:], src)

        def begin(u):
            s, c = divmod(u, CHUNKS)
            if s == STEPS:
                quantize(out_codes[c // 2][:, within(c)], out_scales[:, c * C:(c + 1) * C], grouped[s][c][:])
                if c % 2 == 1:
                    nc.scalar.dma_start(out=word_rows[:, half(c // 2)], in_=out_codes[c // 2][:].bitcast(I32))
                return
            quantize(codes[s][c][:], scales[s][c][:], grouped[s][c][:])
            for g in range(G):
                rows = slice(R * g, R * (g + 1))
                nc.tensor.matmul_mx(
                    out=banks[c % 2][g][:, 0:C],
                    lhsT=w_codes[s][rows, :].bitcast(FP8X4),
                    lhsT_scale=w_scales[s][rows, :],
                    rhs=codes[s][c][rows, :].bitcast(FP8X4),
                    rhs_scale=scales[s][c][rows, :],
                    start=True,
                    stop=True,
                )

        def add(s, c, g):
            nc.vector.tensor_tensor(out=sums[s][c // 2][:, g, within(c)], in0=banks[c % 2][g][:, 0:C],
                                    in1=x_sb[s][c // 2][:, g, within(c)], op=ALU.add)

        def move(s, c, g):
            nc.sync.dma_start(out=moved[s][c][R * g:R * (g + 1), :, :], in_=state[s][c][:, g, :])

        def finish(u):
            s, c = divmod(u, CHUNKS)
            for g in range(G - 1):
                add(s, c, g)
            begin(u + 1)
            add(s, c, G - 1)
            if s < STEPS - 1:
                for g in range(G):
                    nc.vector.tensor_scalar(out=state[s][c][:, g, :], in0=sums[s][c // 2][:, g, within(c)], scalar1=0.0,
                                            scalar2=a_col[:, s, g, 0:1], op0=ALU.max, op1=ALU.mult)
                    move(s, c, g)
            else:
                for g in range(0, G, 2):
                    nc.vector.tensor_scalar(out=state[s][c][:, g:g + 2, :], in0=sums[s][c // 2][:, g:g + 2, within(c)],
                                            scalar1=0.0, scalar2=None, op0=ALU.max)
                    move(s, c, g)
                    move(s, c, g + 1)

        def store_result(i):
            nc.vector.tensor_scalar(out=y_sb[i][:], in0=sums[STEPS - 1][i][:], scalar1=0.0, scalar2=None, op0=ALU.max)
            nc.sync.dma_start(out=out_rows[:, :, half(i)], in_=y_sb[i][:])

        with tc.manual_schedule():
            nc.vector.memset(a_rows[:], 0.0)

            load_w(0)
            nc.scalar.dma_start(out=h_raw[0][:], in_=packed_rows(h)[:, :, half(0)])
            load_x(0, 0)
            for s, a in enumerate((a1, a2)):
                nc.scalar.dma_start(out=a_rows[0:P:R, s, :, :], in_=a.rearrange("g (q i) o -> q g (i o)", i=R))
            nc.scalar.dma_start(out=h_raw[1][:], in_=packed_rows(h)[:, :, half(1)])
            load_x(0, 1)
            load_w(1)

            interleave(True, w_bf[0][:], w_raw[0][:])
            regroup(0, True)
            quantize(w_codes[0][:], w_scales[0][:], w_bf[0][:])
            regroup(1)
            begin(0)
            nc.vector.transpose(out=a_col[:].rearrange("p s g i -> p (s g i)"), in_=a_rows[:].rearrange("p s g i -> p (s g i)"))

            preloads = {0: lambda: load_x(1, 0), 1: lambda: load_w(2), 2: lambda: load_x(1, 1),
                        3: lambda: load_x(2, 0), 5: lambda: load_x(2, 1)}

            for u in range(STEPS * CHUNKS):
                s, c = divmod(u, CHUNKS)
                regroup(u + 2)
                if s < STEPS - 1 and c == 1:
                    interleave(False, w_bf[s + 1][:], w_raw[s + 1][:])
                finish(u)
                if u in preloads:
                    preloads[u]()
                if s < STEPS - 1 and c == 2:
                    quantize(w_codes[s + 1][:], w_scales[s + 1][:], w_bf[s + 1][:])

            last = (STEPS + 1) * CHUNKS - 1
            begin(last - 2)
            store_result(0)
            regroup(last - 1)
            begin(last - 1)
            store_result(1)
            regroup(last, True)
            begin(last)

            for g in range(G):
                queue = nc.sync if g < G - 1 else nc.scalar
                queue.dma_start(out=scale_rows[PACK * g:PACK * (g + 1), :], in_=out_scales[R * g:R * g + PACK, :].bitcast(I32))
